import numpy as np
import ml_dtypes


def mxq(x, axis, fmt="e4m3"):
    dtype, down = {"e4m3": (ml_dtypes.float8_e4m3fn, 7), "e5m2": (ml_dtypes.float8_e5m2, 14)}[fmt]
    v = np.moveaxis(np.asarray(x, np.float32).astype(ml_dtypes.bfloat16).astype(np.float64), axis, -1)
    blocks = v.reshape(v.shape[:-1] + (-1, 32))
    amax = np.abs(blocks).max(-1, keepdims=True)
    byte = np.maximum(np.where(amax > 0, np.frexp(amax)[1] - 1 + 127, 0) - down, 1)
    scale = np.exp2(byte - 127.0)
    codes = (blocks / scale).astype(np.float32).astype(dtype).astype(np.float64)
    return np.moveaxis((codes * scale).reshape(v.shape), -1, axis)


WIDE = False


def mx_kscale(k, group=512):
    if not WIDE:
        return np.ones(k)
    levels = np.array([10, -10, 5, -5, 0])
    if group != 512:
        return np.exp2(np.random.permutation(np.resize(levels, k // group))).repeat(group)
    if k % 512:
        return np.exp2(np.random.permutation(np.resize(levels, k // 32))).repeat(32)
    a = np.empty((k // 512, 16))
    for p in range(k // 512):
        a[p, :8] = np.random.permutation(np.resize(levels, 8))
        for g in range(8):
            far = levels[np.abs(levels - a[p, g]) >= 10]
            a[p, g + 8] = far[np.random.randint(len(far))]
    return np.exp2(a.ravel()).repeat(32)


def f64(x):
    return np.asarray(x).astype(np.float64)


def sigmoid(v):
    return 1.0 / (1.0 + np.exp(-v))


G, D, M, O, N = 2, 256, 128, 256, 512


def setup_inputs():
    n = np.random.standard_normal
    s_d = mx_kscale(D, 0)
    s_o = mx_kscale(O, 0)
    return {
        "x": (n((G, D, N)) * s_d[:, None]).astype(np.float32),
        "w1": (n((G, D, M)) / np.sqrt(D) / s_d[:, None]).astype(np.float32),
        "w2": (n((G, D, M)) / np.sqrt(D) / s_d[:, None]).astype(np.float32),
        "w3": (n((G, D, M)) / np.sqrt(D) / s_d[:, None]).astype(np.float32),
        "wo": (n((G, O, M)) / np.sqrt(O) / s_o[:, None]).astype(np.float32),
        "dy": (n((G, O, N)) * s_o[:, None]).astype(np.float32),
        "og": (np.random.uniform(0.3, 1.0, (G, M, 1))).astype(np.float32),
        "base": (0.2 * n((G, M, N))).astype(np.float32),
    }


def reference(x, w1, w2, w3, wo, dy, og, base):
    w1q = mxq(f64(w1), 1, "e4m3")
    xq = mxq(f64(x), 1, "e4m3")
    z1 = w1q.transpose(0, 2, 1) @ xq
    w2q = mxq(f64(w2), 1, "e4m3")
    z2 = w2q.transpose(0, 2, 1) @ xq
    w3q = mxq(f64(w3), 1, "e4m3")
    z3 = w3q.transpose(0, 2, 1) @ xq
    sg = sigmoid(z1 * z2 + z3)
    woq = mxq(f64(wo), 1, "e4m3")
    dyq = mxq(f64(dy), 1, "e4m3")
    c0 = woq.transpose(0, 2, 1) @ dyq
    dsg = c0 * np.tanh(z3)
    dz3 = c0 * sg * (1.0 - np.square(np.tanh(z3))) + dsg * sg * (1.0 - sg)
    kdz3 = dz3 * 2.0
    kdsg = kdz3 * (1.0 - sg) * sg
    ksg = kdz3 * (1.0 - np.square(np.tanh(z3))) * c0 + kdz3 * (1.0 - sg) * dsg - kdz3 * dsg * sg
    kz3 = kdz3 * c0 * sg * (-1.0) * np.tanh(z3) * 2.0 * (1.0 - np.square(np.tanh(z3))) + kdsg * c0 * (1.0 - np.square(np.tanh(z3))) + ksg * sg * (1.0 - sg)
    y = kz3 * f64(og) + f64(base)
    return y

@@ -1,0 +1,300 @@
+from contextlib import ExitStack
+
+import concourse.mybir as mybir
+
+G, D, M, N = 2, 256, 128, 512
+FLOPS = 4 * 2 * G * D * M * N
+
+F32 = mybir.dt.float32
+BF16 = mybir.dt.bfloat16
+U32 = mybir.dt.uint32
+U8 = mybir.dt.uint8
+FP8X4 = mybir.dt.float8_e4m3fn_x4
+ACT = mybir.ActivationFunctionType
+ALU = mybir.AluOpType
+
+P = 128
+PACK = 4
+ROWS = D // PACK
+NMM = 128
+SPANS = [(0, 128), (128, 256), (256, 512), (0, 256), (256, 384), (384, 512)]
+BOTH = (0, 1)
+
+
+def tile_rows_gpbilinsig_kernel(tc, x, w1, w2, w3, wo, dy, og, base, out):
+    nc = tc.nc
+    with ExitStack() as ctx:
+        sb = ctx.enter_context(tc.tile_pool(name="sb", bufs=1))
+        ps = ctx.enter_context(tc.psum_pool(name="ps", bufs=1))
+        ctx.enter_context(tc.manual_schedule())
+
+        raw = {}
+        grouped = {}
+        mx = {}
+        vals = {}
+
+        def load(name, src, c0, c1):
+            raw[name] = sb.tile([P, PACK, c1 - c0], F32, name=name)
+            nc.sync.dma_start(out=raw[name][:], in_=src.rearrange("g (p j) n -> (g p) j n", j=PACK)[:, :, c0:c1])
+
+        gain = sb.tile([P, G, 8], F32, name="gain")
+        baset = sb.tile([P, G, N], F32, name="baset")
+
+        def load_gain():
+            with nc.allow_non_contiguous_dma(reason="one gain a partition"):
+                nc.sync.dma_start(out=gain[:, :, 0:1], in_=og.rearrange("g p o -> p g o"))
+
+        def load_base():
+            nc.sync.dma_start(out=baset[:], in_=base.rearrange("g p n -> p g n"))
+
+        load("x0", x, 0, 128)
+        load("w2", w2, 0, M)
+        load("w1", w1, 0, M)
+        load("w3", w3, 0, M)
+        load("x1", x, 128, 256)
+        load("x2", x, 256, 512)
+        load("wo", wo, 0, M)
+        load("dya", dy, 0, 256)
+        load_gain()
+        load("dyb", dy, 256, 512)
+        load_base()
+
+        def width(u):
+            return SPANS[u][1] - SPANS[u][0]
+
+        sums = {}
+        for g in BOTH:
+            bank = [ps.tile([P, 512], F32, name="bank%d_%d" % (g, b)) for b in range(4)]
+            sums[("z2", g, 0)] = bank[0][:, 0:128]
+            sums[("z3", g, 0)] = bank[0][:, 128:256]
+            sums[("c", g, 0)] = bank[0][:, 256:384]
+            sums[("c", g, 1)] = bank[0][:, 384:512]
+            sums[("c", g, 3)] = bank[0][:, 256:512]
+            sums[("z1", g, 0)] = bank[1][:, 0:128]
+            sums[("z1", g, 1)] = bank[1][:, 128:256]
+            sums[("z2", g, 1)] = bank[1][:, 256:384]
+            sums[("z3", g, 1)] = bank[1][:, 384:512]
+            sums[("z2", g, 2)] = bank[2][:, 0:256]
+            sums[("z3", g, 2)] = bank[2][:, 256:512]
+            sums[("z1", g, 2)] = bank[3][:, 0:256]
+            sums[("c", g, 2)] = bank[3][:, 256:512]
+
+        def val(name, u, gs):
+            if name not in vals:
+                vals[name] = sb.tile([P, G, N], F32, name=name)
+            if len(gs) == 1:
+                return vals[name][:, gs[0], SPANS[u][0] : SPANS[u][1]]
+            return vals[name][:, :, SPANS[u][0] : SPANS[u][1]]
+
+        def il(name, eng, c0=0, c1=None):
+            w = raw[name].shape[2]
+            if c1 is None:
+                c1 = w
+            if name not in grouped:
+                grouped[name] = sb.tile([P, w, PACK], BF16, name=name + "_bf", align_bytes=64)
+            dst = grouped[name][:, c0:c1, :].rearrange("p (c i) j -> p c j i", i=4)
+            src = raw[name][:, :, c0:c1].rearrange("p j (c i) -> p c j i", i=4)
+            if eng == "V":
+                nc.vector.tensor_copy(out=dst, in_=src)
+            elif eng == "S":
+                nc.scalar.copy(out=dst, in_=src)
+            else:
+                nc.gpsimd.tensor_copy(out=dst, in_=src)
+
+        def q(name, c0=0, c1=None):
+            w = raw[name].shape[2]
+            if c1 is None:
+                c1 = w
+            if name not in mx:
+                codes = sb.tile([P, w], U32, name=name + "_codes", align_bytes=64)
+                scales = sb.tile([P, w], U8, name=name + "_scales", align_bytes=64)
+                mx[name] = (codes, scales)
+            codes, scales = mx[name]
+            nc.vector.quantize_mx(
+                out=codes[:, c0:c1].bitcast(FP8X4),
+                scales=scales[:, c0:c1],
+                in_=grouped[name][:, c0:c1, :].rearrange("p w j -> p (w j)"),
+            )
+
+        def mm(nm, wname, aname, u, a0=0):
+            wc, ws = mx[wname]
+            ac, asc = mx[aname]
+            for g in BOTH:
+                rows = slice(g * ROWS, (g + 1) * ROWS)
+                for c in range(0, width(u), NMM):
+                    nc.tensor.matmul_mx(
+                        out=sums[(nm, g, u)][:, c : c + NMM],
+                        lhsT=wc[rows, :].bitcast(FP8X4),
+                        lhsT_scale=ws[rows, :],
+                        rhs=ac[rows, a0 + c : a0 + c + NMM].bitcast(FP8X4),
+                        rhs_scale=asc[rows, a0 + c : a0 + c + NMM],
+                        start=True,
+                        stop=True,
+                    )
+
+        def stt(o, a, s, b, op0, op1):
+            nc.vector.scalar_tensor_tensor(out=o, in0=a, scalar=s, in1=b, op0=op0, op1=op1)
+
+        def tt(o, a, b, op):
+            nc.vector.tensor_tensor(out=o, in0=a, in1=b, op=op)
+
+        def s_z2(u, gs=BOTH):
+            for g in gs:
+                nc.scalar.copy(out=val("z2", u, [g]), in_=sums[("z2", g, u)])
+
+        def s_t(u, gs=BOTH):
+            for g in gs:
+                nc.scalar.activation(out=val("t", u, [g]), in_=sums[("z3", g, u)], func=ACT.Tanh)
+
+        def s_k(u, gs=BOTH):
+            nc.scalar.activation(out=val("k", u, gs), in_=val("t", u, gs), func=ACT.Square, bias=-0.25)
+
+        def s_h(u, gs=BOTH):
+            nc.scalar.activation(out=val("h", u, gs), in_=val("v", u, gs), func=ACT.Tanh, scale=0.5)
+
+        def s_d(u, gs=BOTH):
+            nc.scalar.activation(out=val("d", u, gs), in_=val("cs", u, gs), func=ACT.Square)
+
+        def v_p(u, gs=BOTH):
+            for g in gs:
+                tt(val("p", u, [g]), sums[("z1", g, u)], val("z2", u, [g]), ALU.mult)
+
+        def v_v(u, gs=BOTH):
+            for g in gs:
+                tt(val("v", u, [g]), sums[("z3", g, u)], val("p", u, [g]), ALU.add)
+
+        def v_g(u, gs=BOTH):
+            stt(val("g", u, gs), val("k", u, gs), -1.0625, val("t", u, gs), ALU.add, ALU.mult)
+
+        def v_w(u, gs=BOTH):
+            stt(val("w", u, gs), val("h", u, gs), -0.5, val("t", u, gs), ALU.mult, ALU.mult)
+
+        def v_a(u, gs=BOTH):
+            stt(val("a", u, gs), val("w", u, gs), 1.0625, val("k", u, gs), ALU.add, ALU.subtract)
+
+        def v_ah(u, gs=BOTH, eng="V"):
+            if eng == "V":
+                tt(val("ah", u, gs), val("a", u, gs), val("h", u, gs), ALU.mult)
+            else:
+                nc.gpsimd.tensor_tensor(out=val("ah", u, gs), in0=val("a", u, gs), in1=val("h", u, gs), op=ALU.mult)
+
+        def v_y(u, gs=BOTH):
+            stt(val("y", u, gs), val("ah", u, gs), -0.5, val("g", u, gs), ALU.mult, ALU.add)
+
+        def v_ab(u, gs=BOTH):
+            stt(val("ab", u, gs), val("y", u, gs), 0.5, val("a", u, gs), ALU.add, ALU.mult)
+
+        def v_cs(u, gs=BOTH):
+            for g in gs:
+                stt(val("cs", u, [g]), val("h", u, [g]), 1.0, sums[("c", g, u)], ALU.add, ALU.mult)
+
+        def v_z(u, gs=BOTH):
+            for g in gs:
+                stt(val("z", u, [g]), val("ab", u, [g]), gain[:, g, 0:1], val("d", u, [g]), ALU.mult, ALU.mult)
+
+        def v_out(u, gs=BOTH, eng="V"):
+            cols = slice(SPANS[u][0], SPANS[u][1])
+            res = val("res", u, gs)
+            zz = val("z", u, gs)
+            bb = baset[:, gs[0], cols] if len(gs) == 1 else baset[:, :, cols]
+            dst = out[gs[0], :, cols] if len(gs) == 1 else out.rearrange("g p n -> p g n")[:, :, cols]
+            if eng == "V":
+                tt(res, zz, bb, ALU.add)
+            else:
+                nc.gpsimd.tensor_tensor(out=res, in0=zz, in1=bb, op=ALU.add)
+            nc.sync.dma_start(out=dst, in_=res)
+
+        il("x0","V")
+        q("x0")
+        il("w2","V")
+        q("w2")
+        mm("z2","w2","x0",0)
+        il("w1","S",64,128)
+        il("w1","V",0,64)
+        q("w1")
+        mm("z1","w1","x0",0)
+        s_z2(0)
+        il("w3","V")
+        q("w3")
+        mm("z3","w3","x0",0)
+        v_p(0)
+        il("x1","S",32,128)
+        il("x1","V",0,32)
+        q("x1")
+        v_v(0)
+        mm("z2","w2","x1",1)
+        mm("z3","w3","x1",1)
+        s_t(0)
+        s_h(0)
+        mm("z1","w1","x1",1)
+        s_k(0)
+        s_z2(1)
+        il("x2","V",0,128)
+        s_t(1)
+        il("x2","S",128,256)
+        v_w(0)
+        v_g(0)
+        v_p(1)
+        v_a(0)
+        v_v(1)
+        s_k(1)
+        s_h(1)
+        q("x2")
+        v_ah(0)
+        mm("z2","w2","x2",2)
+        mm("z3","w3","x2",2)
+        mm("z1","w1","x2",2)
+        il("wo","S")
+        il("dya","S",0,128)
+        s_z2(2)
+        s_t(2)
+        il("dya","S",128,256)
+        v_g(1)
+        v_y(0)
+        v_w(1)
+        v_ab(0)
+        v_a(1)
+        q("wo")
+        v_ah(1)
+        v_p(2,[0])
+        v_y(1)
+        v_p(2,[1])
+        v_v(2,[0])
+        v_ab(1)
+        v_v(2,[1])
+        s_h(2,[0])
+        s_k(2,[0])
+        s_h(2,[1])
+        s_k(2,[1])
+        il("dyb","S")
+        q("dya")
+        mm("c","wo","dya",3)
+        v_w(2,[0])
+        v_g(2,[0])
+        v_w(2,[1])
+        v_a(2,[0])
+        v_cs(3)
+        s_d(3,[0])
+        s_d(3,[1])
+        v_a(2,[1])
+        v_ah(2,[0])
+        v_g(2,[1])
+        q("dyb")
+        mm("c","wo","dyb",2)
+        v_ah(2,[1])
+        v_z(3,[0])
+        v_y(2,[0])
+        v_z(3,[1])
+        v_y(2,[1])
+        v_out(3,[0])
+        v_cs(2,[0])
+        s_d(2,[0])
+        v_cs(2,[1])
+        s_d(2,[1])
+        v_ab(2,[0])
+        v_out(3,[1])
+        v_ab(2,[1])
+        v_z(2,[0])
+        v_z(2,[1])
+        v_out(2,[0])
+        v_out(2,[1])

@@ -16,285 +16,216 @@ ALU = mybir.AluOpType
 P = 128
 PACK = 4
 ROWS = D // PACK
-NMM = 128
-SPANS = [(0, 128), (128, 256), (256, 512), (0, 256), (256, 384), (384, 512)]
-BOTH = (0, 1)
+HALF = N // 2
+N_PASS = 128
+GROUPS = (0, 1)
+X_VECTOR_SHARE = 160
 
 
 def tile_rows_gpbilinsig_kernel(tc, x, w1, w2, w3, wo, dy, og, base, out):
     nc = tc.nc
     with ExitStack() as ctx:
-        sb = ctx.enter_context(tc.tile_pool(name="sb", bufs=1))
-        ps = ctx.enter_context(tc.psum_pool(name="ps", bufs=1))
+        sbuf = ctx.enter_context(tc.tile_pool(name="sbuf", bufs=1))
+        psum = ctx.enter_context(tc.psum_pool(name="psum", bufs=1))
         ctx.enter_context(tc.manual_schedule())
 
         raw = {}
-        grouped = {}
-        mx = {}
-        vals = {}
 
-        def load(name, src, c0, c1):
-            raw[name] = sb.tile([P, PACK, c1 - c0], F32, name=name)
-            nc.sync.dma_start(out=raw[name][:], in_=src.rearrange("g (p j) n -> (g p) j n", j=PACK)[:, :, c0:c1])
+        def load(name, src, first, last):
+            raw[name] = sbuf.tile([P, PACK, last - first], F32, name=name)
+            rows = src.rearrange("g (p j) n -> (g p) j n", j=PACK)
+            nc.sync.dma_start(out=raw[name][:], in_=rows[:, :, first:last])
 
-        gain = sb.tile([P, G, 8], F32, name="gain")
-        baset = sb.tile([P, G, N], F32, name="baset")
-
-        def load_gain():
-            with nc.allow_non_contiguous_dma(reason="one gain a partition"):
-                nc.sync.dma_start(out=gain[:, :, 0:1], in_=og.rearrange("g p o -> p g o"))
-
-        def load_base():
-            nc.sync.dma_start(out=baset[:], in_=base.rearrange("g p n -> p g n"))
-
-        load("x0", x, 0, 128)
+        load("x0", x, 0, HALF)
+        load("w3", w3, 0, M)
         load("w2", w2, 0, M)
         load("w1", w1, 0, M)
-        load("w3", w3, 0, M)
-        load("x1", x, 128, 256)
-        load("x2", x, 256, 512)
+        load("x1", x, HALF, N)
         load("wo", wo, 0, M)
-        load("dya", dy, 0, 256)
-        load_gain()
-        load("dyb", dy, 256, 512)
-        load_base()
-
-        def width(u):
-            return SPANS[u][1] - SPANS[u][0]
+        load("dy0", dy, 0, HALF)
+        load("dy1", dy, HALF, N)
+        gain = sbuf.tile([P, G, 8], F32, name="gain")
+        with nc.allow_non_contiguous_dma(reason="one gain for each partition"):
+            nc.sync.dma_start(out=gain[:, :, 0:1], in_=og.rearrange("g p o -> p g o"))
+        base_sb = sbuf.tile([P, G, N], F32, name="base_sb")
+        nc.sync.dma_start(out=base_sb[:], in_=base.rearrange("g p n -> p g n"))
 
         sums = {}
-        for g in BOTH:
-            bank = [ps.tile([P, 512], F32, name="bank%d_%d" % (g, b)) for b in range(4)]
-            sums[("z2", g, 0)] = bank[0][:, 0:128]
-            sums[("z3", g, 0)] = bank[0][:, 128:256]
-            sums[("c", g, 0)] = bank[0][:, 256:384]
-            sums[("c", g, 1)] = bank[0][:, 384:512]
-            sums[("c", g, 3)] = bank[0][:, 256:512]
-            sums[("z1", g, 0)] = bank[1][:, 0:128]
-            sums[("z1", g, 1)] = bank[1][:, 128:256]
-            sums[("z2", g, 1)] = bank[1][:, 256:384]
-            sums[("z3", g, 1)] = bank[1][:, 384:512]
-            sums[("z2", g, 2)] = bank[2][:, 0:256]
-            sums[("z3", g, 2)] = bank[2][:, 256:512]
-            sums[("z1", g, 2)] = bank[3][:, 0:256]
-            sums[("c", g, 2)] = bank[3][:, 256:512]
+        for g in GROUPS:
+            for pair in ((("z3", 0), ("c0", 0)), (("z2", 0), ("z1", 1)), (("z1", 0), ("c0", 1)), (("z2", 1), ("z3", 1))):
+                bank = psum.tile([P, 2, HALF], F32, name="bank_%d_%s%d" % (g, pair[0][0], pair[0][1]))
+                for place, (name, half) in enumerate(pair):
+                    sums[(name, half, g)] = bank[:, place, :]
 
-        def val(name, u, gs):
-            if name not in vals:
-                vals[name] = sb.tile([P, G, N], F32, name=name)
-            if len(gs) == 1:
-                return vals[name][:, gs[0], SPANS[u][0] : SPANS[u][1]]
-            return vals[name][:, :, SPANS[u][0] : SPANS[u][1]]
+        rounded = {}
+        packed = {}
 
-        def il(name, eng, c0=0, c1=None):
-            w = raw[name].shape[2]
-            if c1 is None:
-                c1 = w
-            if name not in grouped:
-                grouped[name] = sb.tile([P, w, PACK], BF16, name=name + "_bf", align_bytes=64)
-            dst = grouped[name][:, c0:c1, :].rearrange("p (c i) j -> p c j i", i=4)
-            src = raw[name][:, :, c0:c1].rearrange("p j (c i) -> p c j i", i=4)
-            if eng == "V":
-                nc.vector.tensor_copy(out=dst, in_=src)
-            elif eng == "S":
-                nc.scalar.copy(out=dst, in_=src)
-            else:
-                nc.gpsimd.tensor_copy(out=dst, in_=src)
-
-        def q(name, c0=0, c1=None):
-            w = raw[name].shape[2]
-            if c1 is None:
-                c1 = w
-            if name not in mx:
-                codes = sb.tile([P, w], U32, name=name + "_codes", align_bytes=64)
-                scales = sb.tile([P, w], U8, name=name + "_scales", align_bytes=64)
-                mx[name] = (codes, scales)
-            codes, scales = mx[name]
-            nc.vector.quantize_mx(
-                out=codes[:, c0:c1].bitcast(FP8X4),
-                scales=scales[:, c0:c1],
-                in_=grouped[name][:, c0:c1, :].rearrange("p w j -> p (w j)"),
+        def round_and_pack(name, copy, first, last):
+            if name not in rounded:
+                rounded[name] = sbuf.tile([P, raw[name].shape[2], PACK], BF16, name=name + "_bf16", align_bytes=64)
+            copy(
+                out=rounded[name][:, first:last, :].rearrange("p (c i) j -> p c j i", i=2),
+                in_=raw[name][:, :, first:last].rearrange("p j (c i) -> p c j i", i=2),
             )
 
-        def mm(nm, wname, aname, u, a0=0):
-            wc, ws = mx[wname]
-            ac, asc = mx[aname]
-            for g in BOTH:
+        def quantise(name):
+            width = raw[name].shape[2]
+            codes = sbuf.tile([P, width], U32, name=name + "_codes", align_bytes=64)
+            scales = sbuf.tile([P, width], U8, name=name + "_scales", align_bytes=64)
+            nc.vector.quantize_mx(
+                out=codes[:].bitcast(FP8X4), scales=scales[:], in_=rounded[name][:].rearrange("p w j -> p (w j)")
+            )
+            packed[name] = (codes, scales)
+
+        def product(name, half, weights, moving, groups=GROUPS):
+            w_codes, w_scales = packed[weights]
+            m_codes, m_scales = packed[moving]
+            for g in groups:
                 rows = slice(g * ROWS, (g + 1) * ROWS)
-                for c in range(0, width(u), NMM):
+                for first in range(0, HALF, N_PASS):
+                    cols = slice(first, first + N_PASS)
                     nc.tensor.matmul_mx(
-                        out=sums[(nm, g, u)][:, c : c + NMM],
-                        lhsT=wc[rows, :].bitcast(FP8X4),
-                        lhsT_scale=ws[rows, :],
-                        rhs=ac[rows, a0 + c : a0 + c + NMM].bitcast(FP8X4),
-                        rhs_scale=asc[rows, a0 + c : a0 + c + NMM],
+                        out=sums[(name, half, g)][:, cols],
+                        lhsT=w_codes[rows, :].bitcast(FP8X4),
+                        lhsT_scale=w_scales[rows, :],
+                        rhs=m_codes[rows, cols].bitcast(FP8X4),
+                        rhs_scale=m_scales[rows, cols],
                         start=True,
                         stop=True,
                     )
 
-        def stt(o, a, s, b, op0, op1):
-            nc.vector.scalar_tensor_tensor(out=o, in0=a, scalar=s, in1=b, op0=op0, op1=op1)
+        values = {}
 
-        def tt(o, a, b, op):
-            nc.vector.tensor_tensor(out=o, in0=a, in1=b, op=op)
+        def part(tile, half, g):
+            cols = slice(half * HALF, (half + 1) * HALF)
+            return tile[:, :, cols] if g is None else tile[:, g, cols]
 
-        def s_z2(u, gs=BOTH):
-            for g in gs:
-                nc.scalar.copy(out=val("z2", u, [g]), in_=sums[("z2", g, u)])
+        def val(name, half, g):
+            if name not in values:
+                values[name] = sbuf.tile([P, 2, G, HALF], F32, name=name)
+            return values[name][:, half, :, :] if g is None else values[name][:, half, g, :]
 
-        def s_t(u, gs=BOTH):
-            for g in gs:
-                nc.scalar.activation(out=val("t", u, [g]), in_=sums[("z3", g, u)], func=ACT.Tanh)
+        def fused(result, in0, scalar, in1, op0, op1):
+            nc.vector.scalar_tensor_tensor(out=result, in0=in0, scalar=scalar, in1=in1, op0=op0, op1=op1)
 
-        def s_k(u, gs=BOTH):
-            nc.scalar.activation(out=val("k", u, gs), in_=val("t", u, gs), func=ACT.Square, bias=-0.25)
+        def copy_z2(half, g):
+            nc.scalar.copy(out=val("z2", half, g), in_=sums[("z2", half, g)])
 
-        def s_h(u, gs=BOTH):
-            nc.scalar.activation(out=val("h", u, gs), in_=val("v", u, gs), func=ACT.Tanh, scale=0.5)
+        def make_t(half, g):
+            nc.scalar.activation(out=val("t", half, g), in_=sums[("z3", half, g)], func=ACT.Tanh)
 
-        def s_d(u, gs=BOTH):
-            nc.scalar.activation(out=val("d", u, gs), in_=val("cs", u, gs), func=ACT.Square)
+        def make_sq(half, g):
+            nc.scalar.activation(out=val("sq", half, g), in_=val("t", half, g), func=ACT.Square, bias=-0.25)
 
-        def v_p(u, gs=BOTH):
-            for g in gs:
-                tt(val("p", u, [g]), sums[("z1", g, u)], val("z2", u, [g]), ALU.mult)
+        def make_z12(half, g):
+            nc.vector.tensor_tensor(out=val("z12", half, g), in0=sums[("z1", half, g)], in1=val("z2", half, g), op=ALU.mult)
 
-        def v_v(u, gs=BOTH):
-            for g in gs:
-                tt(val("v", u, [g]), sums[("z3", g, u)], val("p", u, [g]), ALU.add)
+        def make_h(half, g):
+            nc.vector.tensor_tensor(out=val("v", half, g), in0=sums[("z3", half, g)], in1=val("z12", half, g), op=ALU.add)
+            nc.scalar.activation(out=val("h", half, g), in_=val("v", half, g), func=ACT.Tanh, scale=0.5)
 
-        def v_g(u, gs=BOTH):
-            stt(val("g", u, gs), val("k", u, gs), -1.0625, val("t", u, gs), ALU.add, ALU.mult)
+        def make_cub(half, g):
+            fused(val("cub", half, g), val("sq", half, g), -1.0625, val("t", half, g), ALU.add, ALU.mult)
 
-        def v_w(u, gs=BOTH):
-            stt(val("w", u, gs), val("h", u, gs), -0.5, val("t", u, gs), ALU.mult, ALU.mult)
+        def make_ht(half, g):
+            fused(val("ht", half, g), val("h", half, g), -0.5, val("t", half, g), ALU.mult, ALU.mult)
 
-        def v_a(u, gs=BOTH):
-            stt(val("a", u, gs), val("w", u, gs), 1.0625, val("k", u, gs), ALU.add, ALU.subtract)
+        def make_a(half, g):
+            fused(val("a", half, g), val("ht", half, g), 1.0625, val("sq", half, g), ALU.add, ALU.subtract)
 
-        def v_ah(u, gs=BOTH, eng="V"):
-            if eng == "V":
-                tt(val("ah", u, gs), val("a", u, gs), val("h", u, gs), ALU.mult)
-            else:
-                nc.gpsimd.tensor_tensor(out=val("ah", u, gs), in0=val("a", u, gs), in1=val("h", u, gs), op=ALU.mult)
+        def make_ah(half):
+            nc.gpsimd.tensor_tensor(out=val("ah", half, None), in0=val("a", half, None), in1=val("h", half, None), op=ALU.mult)
 
-        def v_y(u, gs=BOTH):
-            stt(val("y", u, gs), val("ah", u, gs), -0.5, val("g", u, gs), ALU.mult, ALU.add)
+        def make_b0(half, g):
+            fused(val("b0", half, g), val("ah", half, g), -0.5, val("cub", half, g), ALU.mult, ALU.add)
 
-        def v_ab(u, gs=BOTH):
-            stt(val("ab", u, gs), val("y", u, gs), 0.5, val("a", u, gs), ALU.add, ALU.mult)
+        def make_ab(half, g):
+            fused(val("ab", half, g), val("b0", half, g), 0.5, val("a", half, g), ALU.add, ALU.mult)
 
-        def v_cs(u, gs=BOTH):
-            for g in gs:
-                stt(val("cs", u, [g]), val("h", u, [g]), 1.0, sums[("c", g, u)], ALU.add, ALU.mult)
+        def make_hc(half, g):
+            fused(val("hc", half, g), val("h", half, g), 1.0, sums[("c0", half, g)], ALU.add, ALU.mult)
 
-        def v_z(u, gs=BOTH):
-            for g in gs:
-                stt(val("z", u, [g]), val("ab", u, [g]), gain[:, g, 0:1], val("d", u, [g]), ALU.mult, ALU.mult)
+        def make_hc2(half, g):
+            nc.scalar.activation(out=val("hc2", half, g), in_=val("hc", half, g), func=ACT.Square)
 
-        def v_out(u, gs=BOTH, eng="V"):
-            cols = slice(SPANS[u][0], SPANS[u][1])
-            res = val("res", u, gs)
-            zz = val("z", u, gs)
-            bb = baset[:, gs[0], cols] if len(gs) == 1 else baset[:, :, cols]
-            dst = out[gs[0], :, cols] if len(gs) == 1 else out.rearrange("g p n -> p g n")[:, :, cols]
-            if eng == "V":
-                tt(res, zz, bb, ALU.add)
-            else:
-                nc.gpsimd.tensor_tensor(out=res, in0=zz, in1=bb, op=ALU.add)
-            nc.sync.dma_start(out=dst, in_=res)
+        def make_term(half, g):
+            fused(val("term", half, g), val("ab", half, g), gain[:, g, 0:1], val("hc2", half, g), ALU.mult, ALU.mult)
 
-        il("x0","V")
-        q("x0")
-        il("w2","V")
-        q("w2")
-        mm("z2","w2","x0",0)
-        il("w1","S",64,128)
-        il("w1","V",0,64)
-        q("w1")
-        mm("z1","w1","x0",0)
-        s_z2(0)
-        il("w3","V")
-        q("w3")
-        mm("z3","w3","x0",0)
-        v_p(0)
-        il("x1","S",32,128)
-        il("x1","V",0,32)
-        q("x1")
-        v_v(0)
-        mm("z2","w2","x1",1)
-        mm("z3","w3","x1",1)
-        s_t(0)
-        s_h(0)
-        mm("z1","w1","x1",1)
-        s_k(0)
-        s_z2(1)
-        il("x2","V",0,128)
-        s_t(1)
-        il("x2","S",128,256)
-        v_w(0)
-        v_g(0)
-        v_p(1)
-        v_a(0)
-        v_v(1)
-        s_k(1)
-        s_h(1)
-        q("x2")
-        v_ah(0)
-        mm("z2","w2","x2",2)
-        mm("z3","w3","x2",2)
-        mm("z1","w1","x2",2)
-        il("wo","S")
-        il("dya","S",0,128)
-        s_z2(2)
-        s_t(2)
-        il("dya","S",128,256)
-        v_g(1)
-        v_y(0)
-        v_w(1)
-        v_ab(0)
-        v_a(1)
-        q("wo")
-        v_ah(1)
-        v_p(2,[0])
-        v_y(1)
-        v_p(2,[1])
-        v_v(2,[0])
-        v_ab(1)
-        v_v(2,[1])
-        s_h(2,[0])
-        s_k(2,[0])
-        s_h(2,[1])
-        s_k(2,[1])
-        il("dyb","S")
-        q("dya")
-        mm("c","wo","dya",3)
-        v_w(2,[0])
-        v_g(2,[0])
-        v_w(2,[1])
-        v_a(2,[0])
-        v_cs(3)
-        s_d(3,[0])
-        s_d(3,[1])
-        v_a(2,[1])
-        v_ah(2,[0])
-        v_g(2,[1])
-        q("dyb")
-        mm("c","wo","dyb",2)
-        v_ah(2,[1])
-        v_z(3,[0])
-        v_y(2,[0])
-        v_z(3,[1])
-        v_y(2,[1])
-        v_out(3,[0])
-        v_cs(2,[0])
-        s_d(2,[0])
-        v_cs(2,[1])
-        s_d(2,[1])
-        v_ab(2,[0])
-        v_out(3,[1])
-        v_ab(2,[1])
-        v_z(2,[0])
-        v_z(2,[1])
-        v_out(2,[0])
-        v_out(2,[1])
+        def finish(half, g):
+            result = val("result", half, g)
+            nc.vector.tensor_tensor(out=result, in0=val("term", half, g), in1=part(base_sb, half, g), op=ALU.add)
+            nc.sync.dma_start(out=part(out.rearrange("g p n -> p g n"), half, g), in_=result)
+
+        def each_group(step, half):
+            for g in GROUPS:
+                step(half, g)
+
+        on_vector = nc.vector.tensor_copy
+        on_scalar = nc.scalar.copy
+
+        round_and_pack("x0", on_vector, 0, X_VECTOR_SHARE)
+        round_and_pack("x0", on_scalar, X_VECTOR_SHARE, HALF)
+        round_and_pack("w3", on_vector, 0, M)
+        quantise("x0")
+        quantise("w3")
+        product("z3", 0, "w3", "x0")
+        for name, result in (("w2", "z2"), ("w1", "z1")):
+            round_and_pack(name, on_scalar, M // 2, M)
+            round_and_pack(name, on_vector, 0, M // 2)
+            quantise(name)
+            product(result, 0, name, "x0")
+        each_group(make_t, 0)
+        each_group(copy_z2, 0)
+        round_and_pack("x1", on_vector, 0, HALF)
+        make_sq(0, None)
+        round_and_pack("wo", on_scalar, 0, M)
+
+        make_z12(0, 0)
+        quantise("x1")
+        for g in GROUPS:
+            product("z2", 1, "w2", "x1", [g])
+            product("z3", 1, "w3", "x1", [g])
+        product("z1", 1, "w1", "x1")
+        make_z12(0, 1)
+        each_group(make_h, 0)
+        make_cub(0, 0)
+        quantise("wo")
+        each_group(copy_z2, 1)
+        each_group(make_t, 1)
+        each_group(make_sq, 1)
+        round_and_pack("dy0", on_scalar, 0, HALF // 2)
+        each_group(make_ht, 0)
+        each_group(make_a, 0)
+
+        make_ah(0)
+        make_cub(0, 1)
+        each_group(make_z12, 1)
+        each_group(make_h, 1)
+        round_and_pack("dy0", on_scalar, HALF // 2, HALF)
+        round_and_pack("dy1", on_scalar, 0, HALF)
+
+        make_cub(1, None)
+        make_b0(0, None)
+        each_group(make_ht, 1)
+        quantise("dy0")
+        product("c0", 0, "wo", "dy0")
+        make_a(1, 0)
+        make_ab(0, 0)
+        quantise("dy1")
+        product("c0", 1, "wo", "dy1")
+        make_a(1, 1)
+
+        make_ah(1)
+        make_ab(0, 1)
+        for g in GROUPS:
+            make_hc(0, g)
+            make_hc2(0, g)
+        each_group(make_hc, 1)
+        make_hc2(1, None)
+
+        each_group(make_term, 0)
+        make_b0(1, None)
+        finish(0, None)
+        each_group(make_ab, 1)
+        each_group(make_term, 1)
+        each_group(finish, 1)

@@ -64,8 +64,8 @@ def tile_rows_gpbilinsig_kernel(tc, x, w1, w2, w3, wo, dy, og, base, out):
             if name not in rounded:
                 rounded[name] = sbuf.tile([P, raw[name].shape[2], PACK], BF16, name=name + "_bf16", align_bytes=64)
             copy(
-                out=rounded[name][:, first:last, :].rearrange("p (c i) j -> p c j i", i=2),
-                in_=raw[name][:, :, first:last].rearrange("p j (c i) -> p c j i", i=2),
+                out=rounded[name][:, first:last, :].rearrange("p (c i) j -> p c j i", i=4),
+                in_=raw[name][:, :, first:last].rearrange("p j (c i) -> p c j i", i=4),
             )
 
         def quantise(name):

from contextlib import ExitStack

import concourse.mybir as mybir

G, D, M, N = 2, 256, 128, 512
FLOPS = 4 * 2 * G * D * M * N

F32 = mybir.dt.float32
BF16 = mybir.dt.bfloat16
U32 = mybir.dt.uint32
U8 = mybir.dt.uint8
FP8X4 = mybir.dt.float8_e4m3fn_x4
ACT = mybir.ActivationFunctionType
ALU = mybir.AluOpType

P = 128
PACK = 4
ROWS = D // PACK
HALF = N // 2
N_PASS = 128
GROUPS = (0, 1)
X_VECTOR_SHARE = 160


def tile_rows_gpbilinsig_kernel(tc, x, w1, w2, w3, wo, dy, og, base, out):
    nc = tc.nc
    with ExitStack() as ctx:
        sbuf = ctx.enter_context(tc.tile_pool(name="sbuf", bufs=1))
        psum = ctx.enter_context(tc.psum_pool(name="psum", bufs=1))
        ctx.enter_context(tc.manual_schedule())

        raw = {}

        def load(name, src, first, last):
            raw[name] = sbuf.tile([P, PACK, last - first], F32, name=name)
            rows = src.rearrange("g (p j) n -> (g p) j n", j=PACK)
            nc.sync.dma_start(out=raw[name][:], in_=rows[:, :, first:last])

        load("x0", x, 0, HALF)
        load("w3", w3, 0, M)
        load("w2", w2, 0, M)
        load("w1", w1, 0, M)
        load("x1", x, HALF, N)
        load("wo", wo, 0, M)
        load("dy0", dy, 0, HALF)
        load("dy1", dy, HALF, N)
        gain = sbuf.tile([P, G, 8], F32, name="gain")
        with nc.allow_non_contiguous_dma(reason="one gain for each partition"):
            nc.sync.dma_start(out=gain[:, :, 0:1], in_=og.rearrange("g p o -> p g o"))
        base_sb = sbuf.tile([P, G, N], F32, name="base_sb")
        nc.sync.dma_start(out=base_sb[:], in_=base.rearrange("g p n -> p g n"))

        sums = {}
        for g in GROUPS:
            for pair in ((("z3", 0), ("c0", 0)), (("z2", 0), ("z1", 1)), (("z1", 0), ("c0", 1)), (("z2", 1), ("z3", 1))):
                bank = psum.tile([P, 2, HALF], F32, name="bank_%d_%s%d" % (g, pair[0][0], pair[0][1]))
                for place, (name, half) in enumerate(pair):
                    sums[(name, half, g)] = bank[:, place, :]

        rounded = {}
        packed = {}

        def round_and_pack(name, copy, first, last):
            if name not in rounded:
                rounded[name] = sbuf.tile([P, raw[name].shape[2], PACK], BF16, name=name + "_bf16", align_bytes=64)
            copy(
                out=rounded[name][:, first:last, :].rearrange("p (c i) j -> p c j i", i=4),
                in_=raw[name][:, :, first:last].rearrange("p j (c i) -> p c j i", i=4),
            )

        def quantise(name):
            width = raw[name].shape[2]
            codes = sbuf.tile([P, width], U32, name=name + "_codes", align_bytes=64)
            scales = sbuf.tile([P, width], U8, name=name + "_scales", align_bytes=64)
            nc.vector.quantize_mx(
                out=codes[:].bitcast(FP8X4), scales=scales[:], in_=rounded[name][:].rearrange("p w j -> p (w j)")
            )
            packed[name] = (codes, scales)

        def product(name, half, weights, moving, groups=GROUPS):
            w_codes, w_scales = packed[weights]
            m_codes, m_scales = packed[moving]
            for g in groups:
                rows = slice(g * ROWS, (g + 1) * ROWS)
                for first in range(0, HALF, N_PASS):
                    cols = slice(first, first + N_PASS)
                    nc.tensor.matmul_mx(
                        out=sums[(name, half, g)][:, cols],
                        lhsT=w_codes[rows, :].bitcast(FP8X4),
                        lhsT_scale=w_scales[rows, :],
                        rhs=m_codes[rows, cols].bitcast(FP8X4),
                        rhs_scale=m_scales[rows, cols],
                        start=True,
                        stop=True,
                    )

        values = {}

        def part(tile, half, g):
            cols = slice(half * HALF, (half + 1) * HALF)
            return tile[:, :, cols] if g is None else tile[:, g, cols]

        def val(name, half, g):
            if name not in values:
                values[name] = sbuf.tile([P, 2, G, HALF], F32, name=name)
            return values[name][:, half, :, :] if g is None else values[name][:, half, g, :]

        def fused(result, in0, scalar, in1, op0, op1):
            nc.vector.scalar_tensor_tensor(out=result, in0=in0, scalar=scalar, in1=in1, op0=op0, op1=op1)

        def copy_z2(half, g):
            nc.scalar.copy(out=val("z2", half, g), in_=sums[("z2", half, g)])

        def make_t(half, g):
            nc.scalar.activation(out=val("t", half, g), in_=sums[("z3", half, g)], func=ACT.Tanh)

        def make_sq(half, g):
            nc.scalar.activation(out=val("sq", half, g), in_=val("t", half, g), func=ACT.Square, bias=-0.25)

        def make_z12(half, g):
            nc.vector.tensor_tensor(out=val("z12", half, g), in0=sums[("z1", half, g)], in1=val("z2", half, g), op=ALU.mult)

        def make_h(half, g):
            nc.vector.tensor_tensor(out=val("v", half, g), in0=sums[("z3", half, g)], in1=val("z12", half, g), op=ALU.add)
            nc.scalar.activation(out=val("h", half, g), in_=val("v", half, g), func=ACT.Tanh, scale=0.5)

        def make_cub(half, g):
            fused(val("cub", half, g), val("sq", half, g), -1.0625, val("t", half, g), ALU.add, ALU.mult)

        def make_ht(half, g):
            fused(val("ht", half, g), val("h", half, g), -0.5, val("t", half, g), ALU.mult, ALU.mult)

        def make_a(half, g):
            fused(val("a", half, g), val("ht", half, g), 1.0625, val("sq", half, g), ALU.add, ALU.subtract)

        def make_ah(half):
            nc.gpsimd.tensor_tensor(out=val("ah", half, None), in0=val("a", half, None), in1=val("h", half, None), op=ALU.mult)

        def make_b0(half, g):
            fused(val("b0", half, g), val("ah", half, g), -0.5, val("cub", half, g), ALU.mult, ALU.add)

        def make_ab(half, g):
            fused(val("ab", half, g), val("b0", half, g), 0.5, val("a", half, g), ALU.add, ALU.mult)

        def make_hc(half, g):
            fused(val("hc", half, g), val("h", half, g), 1.0, sums[("c0", half, g)], ALU.add, ALU.mult)

        def make_hc2(half, g):
            nc.scalar.activation(out=val("hc2", half, g), in_=val("hc", half, g), func=ACT.Square)

        def make_term(half, g):
            fused(val("term", half, g), val("ab", half, g), gain[:, g, 0:1], val("hc2", half, g), ALU.mult, ALU.mult)

        def finish(half, g):
            result = val("result", half, g)
            nc.vector.tensor_tensor(out=result, in0=val("term", half, g), in1=part(base_sb, half, g), op=ALU.add)
            nc.sync.dma_start(out=part(out.rearrange("g p n -> p g n"), half, g), in_=result)

        def each_group(step, half):
            for g in GROUPS:
                step(half, g)

        on_vector = nc.vector.tensor_copy
        on_scalar = nc.scalar.copy

        round_and_pack("x0", on_vector, 0, X_VECTOR_SHARE)
        round_and_pack("x0", on_scalar, X_VECTOR_SHARE, HALF)
        round_and_pack("w3", on_vector, 0, M)
        quantise("x0")
        quantise("w3")
        product("z3", 0, "w3", "x0")
        for name, result in (("w2", "z2"), ("w1", "z1")):
            round_and_pack(name, on_scalar, M // 2, M)
            round_and_pack(name, on_vector, 0, M // 2)
            quantise(name)
            product(result, 0, name, "x0")
        each_group(make_t, 0)
        each_group(copy_z2, 0)
        round_and_pack("x1", on_vector, 0, HALF)
        make_sq(0, None)
        round_and_pack("wo", on_scalar, 0, M)

        make_z12(0, 0)
        quantise("x1")
        for g in GROUPS:
            product("z2", 1, "w2", "x1", [g])
            product("z3", 1, "w3", "x1", [g])
        product("z1", 1, "w1", "x1")
        make_z12(0, 1)
        each_group(make_h, 0)
        make_cub(0, 0)
        quantise("wo")
        each_group(copy_z2, 1)
        each_group(make_t, 1)
        each_group(make_sq, 1)
        round_and_pack("dy0", on_scalar, 0, HALF // 2)
        each_group(make_ht, 0)
        each_group(make_a, 0)

        make_ah(0)
        make_cub(0, 1)
        each_group(make_z12, 1)
        each_group(make_h, 1)
        round_and_pack("dy0", on_scalar, HALF // 2, HALF)
        round_and_pack("dy1", on_scalar, 0, HALF)

        make_cub(1, None)
        make_b0(0, None)
        each_group(make_ht, 1)
        quantise("dy0")
        product("c0", 0, "wo", "dy0")
        make_a(1, 0)
        make_ab(0, 0)
        quantise("dy1")
        product("c0", 1, "wo", "dy1")
        make_a(1, 1)

        make_ah(1)
        make_ab(0, 1)
        for g in GROUPS:
            make_hc(0, g)
            make_hc2(0, g)
        each_group(make_hc, 1)
        make_hc2(1, None)

        each_group(make_term, 0)
        make_b0(1, None)
        finish(0, None)
        each_group(make_ab, 1)
        each_group(make_term, 1)
        each_group(finish, 1)
